import numpy as np, ml_dtypes
CORES = [6,14,22,30,38,134,142,150,158]
N = 9
F = 512
def setup_inputs(rng):
    x = (rng.standard_normal((N, 128, 128), dtype=np.float32) / 11).astype(ml_dtypes.bfloat16)
    w = rng.standard_normal((128, F), dtype=np.float32).astype(ml_dtypes.bfloat16)
    return {"x": x, "xt": x.transpose(0, 2, 1).copy(), "w": np.broadcast_to(w, (N, 128, F)).copy()}
def setup_inputs_big(rng):
    d = setup_inputs(rng)
    for k in ("x", "xt", "w"): d[k] = (d[k].astype(np.float32) * 1024.0).astype(d[k].dtype)
    return d
def setup_inputs_small(rng):
    d = setup_inputs(rng)
    for k in ("x", "xt", "w"): d[k] = (d[k].astype(np.float32) * (1 / 1024.0)).astype(d[k].dtype)
    return d
def setup_inputs_apart(rng):
    d = setup_inputs(rng)
    f = (10.0 ** rng.permutation(np.linspace(-1.5, 1.5, N))).astype(np.float32).reshape(N, 1, 1)
    for k in ("x", "xt"): d[k] = (d[k].astype(np.float32) * f).astype(d[k].dtype)
    return d
def reference(x, xt, w):
    X, XT, W = x.astype(np.float64), xt.astype(np.float64), w.astype(np.float64)
    s = sum(X[j].T @ (XT[j].T @ W[j]) for j in range(N)).astype(ml_dtypes.bfloat16)
    return {"y": np.broadcast_to(s, (N,) + s.shape)}

from concourse.bass import DstId, RemoteDMATransfer

P = 128
D = 128
F = 512
H = F // 2
GROUPS = (("d", 4), ("d", 2), ("s", 2))
TENSOR_ORDER = (0, 2, 1)

SCRATCH = {
    "xd": ("dram", [P, D], "bfloat16"),
    "xs": ("sbuf", [P, D], "bfloat16"),
    "ws": ("sbuf", [P, F], "bfloat16"),
    "gs": ("sbuf", [P, D], "bfloat16"),
    "ys": ("sbuf", [P, F], "bfloat16"),
    "gp": ("psum", [P, 512], "float32"),
    "yp0": ("psum", [P, 512], "float32"),
    "yp1": ("psum", [P, 512], "float32"),
}
SEMAPHORES = ["xd", "xs", "w", "sent", "gsum", "gcopy", "mm0", "mm1", "cp0", "cp1", "st0", "st1"]
for _i, (_kind, _cnt) in enumerate(GROUPS):
    SEMAPHORES.append("arr%d" % _i)
    SCRATCH["tile%d" % _i] = ("sbuf", [P, _cnt * D], "bfloat16")
    if _kind == "d":
        SCRATCH["land%d" % _i] = ("dram", [_cnt, P, D], "bfloat16")
        SEMAPHORES.append("rdy%d" % _i)


def rank_program(g, core, T, topo):
    rank = T.rank_of(core)
    if rank is None:
        return
    S = T.sem
    cores = T.cores
    n = len(cores)

    g.sync.dma_start(T.xd[:, :], T.x[:, :]).then_inc(S.xd, 16)
    g.scalar.dma_start(T.xs[:, :], T.x[:, :]).then_inc(S.xs, 16)
    g.scalar.dma_start(T.ws[:, :], T.w[:, :]).then_inc(S.w, 16)

    g.wait_ge(S.xd, 16)
    off = 1
    sent = 0
    arrive = []
    for i, (kind, cnt) in enumerate(GROUPS):
        dst_cores = [cores[(rank + off + k) % n] for k in range(cnt)]
        mask = topo.mask(core, dst_cores[0])
        for d in dst_cores:
            assert topo.may_write(core, d)
            mask &= topo.mask(core, d)
        engines = bin(mask).count("1")
        ids = []
        for d in dst_cores:
            rid, pid = topo.addr(d, core)
            ids.append(DstId(rid=rid, pnc=pid))
        if kind == "d":
            outs = [T["land%d" % i][k] for k in range(cnt)]
        else:
            outs = [T["tile%d" % i][:, k * D:(k + 1) * D] for k in range(cnt)]
        g.remote_dma_fused(
            [RemoteDMATransfer(dst_ids=ids, dma_engine_mask=mask, remote_sem=S["arr%d" % i],
                               srcs=[T.xd[:, :]], dsts=outs, alu_op=0)],
            local_sem=S.sent)
        sent += engines
        arrive.append(cnt * engines)
        off += cnt

    queues = [g.sync, g.scalar]
    nd = 0
    ready = []
    for i, (kind, cnt) in enumerate(GROUPS):
        if kind == "d":
            q = queues[nd % 2]
            nd += 1
            q.wait_ge(S["arr%d" % i], arrive[i])
            q.dma_start(T["tile%d" % i][:, :], T["land%d" % i][:]).then_inc(S["rdy%d" % i], 16)
            ready.append((S["rdy%d" % i], 16))
        else:
            ready.append((S["arr%d" % i], arrive[i]))

    te, ve = g.tensor, g.vector
    G = T.gp[:, 0:D]
    te.wait_ge(S.xs, 16)
    te.matmul(G, T.xs[:, :], T.xs[:, :], True, False)
    left = n - 1
    for i in TENSOR_ORDER:
        te.wait_ge(ready[i][0], ready[i][1])
        for k in range(GROUPS[i][1]):
            blk = T["tile%d" % i][:, k * D:(k + 1) * D]
            left -= 1
            mm = te.matmul(G, blk, blk, False, left == 0)
    mm.then_inc(S.gsum, 1)

    ve.wait_ge(S.gsum, 1)
    ve.tensor_copy(T.gs[:, :], G).then_inc(S.gcopy, 1)

    te.wait_ge(S.w, 16)
    te.wait_ge(S.gcopy, 1)
    te.matmul(T.yp0[:, 0:H], T.gs[:, :], T.ws[:, 0:H], True, True).then_inc(S.mm0, 1)
    te.matmul(T.yp1[:, 0:H], T.gs[:, :], T.ws[:, H:F], True, True).then_inc(S.mm1, 1)
    ve.wait_ge(S.mm0, 1)
    ve.tensor_copy(T.ys[:, 0:H], T.yp0[:, 0:H]).then_inc(S.cp0, 1)
    ve.wait_ge(S.mm1, 1)
    ve.tensor_copy(T.ys[:, H:F], T.yp1[:, 0:H]).then_inc(S.cp1, 1)
    g.sync.wait_ge(S.cp0, 1)
    g.sync.dma_start(T.y[:, 0:H], T.ys[:, 0:H]).then_inc(S.st0, 16)
    g.scalar.wait_ge(S.cp1, 1)
    g.scalar.dma_start(T.y[:, H:F], T.ys[:, H:F]).then_inc(S.st1, 16)

    g.wait_ge(S.sent, sent)
    g.wait_ge(S.st0, 16)
    g.wait_ge(S.st1, 16)
